import numpy as np
import ml_dtypes

BF16 = ml_dtypes.bfloat16


def bf(x):
    return np.asarray(x, np.float32).astype(BF16)


def f32(x):
    return np.asarray(x, np.float32)


def f64(x):
    return np.asarray(x).astype(np.float64)


def striped(idx):
    return np.concatenate([l.reshape(-1, 16).T for l in idx])


def rows(idx, k):
    return np.tile(np.repeat(idx, 16, axis=0), (k // (16 * 8), 1))


def look(tab, idx):
    return np.take_along_axis(f64(tab), rows(idx, len(tab)), axis=1)


P, K, S, R, V, N = 128, 512, 2048, 4, 2048, 2048


def setup_inputs():
    return {"tab": f32(0.5 * np.random.standard_normal((K, S))), "u": f32(0.3 * np.random.standard_normal((K, V))), "e": bf(np.tile(np.eye(16), (8, 1))), "mg": f32(np.random.standard_normal((16 * R, 1))), "offs": striped(np.random.randint(0, S, (8, N)))}


def reference(tab, u, e, mg, offs):
    idx = np.stack([g.T.reshape(-1) for g in np.split(offs, 8)])
    s = look(tab, idx) + f64(u)
    s = np.concatenate([f64(e).T @ s[a:a + P] for a in range(0, K, P)])
    x = np.maximum(f64(mg) - s, 0.0)
    return x

@@ -1,0 +1,67 @@
+import concourse.mybir as mybir
+
+F32, BF16, U16 = mybir.dt.float32, mybir.dt.bfloat16, mybir.dt.uint16
+ADD = mybir.AluOpType.add
+RELU = mybir.ActivationFunctionType.Relu
+
+P = 128
+QUERIES = 16
+PIECE = 512
+
+FLOPS = 2 * 512 * 2048 + 2 * 64 * 2048
+
+
+def tile_lookup_adc_best_out_kernel(tc, tab, u, e, mg, offs, out):
+    nc = tc.nc
+    rows, codewords = tab.shape
+    vectors = u.shape[1]
+    blocks = rows // P
+    pieces = vectors // PIECE
+    queries = blocks * QUERIES
+    list_columns = PIECE // 16
+
+    with (
+        tc.tile_pool(name="held", bufs=1) as held,
+        tc.tile_pool(name="ring", bufs=4) as ring,
+        tc.psum_pool(name="psum", bufs=1) as psum,
+    ):
+        lists = held.tile([P, vectors // 16], U16)
+        nc.sync.dma_start(lists[:], offs)
+
+        tables = []
+        corrections = []
+        for b in range(blocks):
+            table = held.tile([P, codewords], F32, name=f"table{b}")
+            nc.sync.dma_start(table[:], tab[b * P : (b + 1) * P, :])
+            correction = held.tile([P, vectors], F32, name=f"correction{b}")
+            for i in range(pieces):
+                cols = slice(i * PIECE, (i + 1) * PIECE)
+                nc.sync.dma_start(correction[:, cols], u[b * P : (b + 1) * P, cols])
+            tables.append(table)
+            corrections.append(correction)
+
+        lead = queries - QUERIES
+        padded_e = held.tile([P, lead + queries], BF16)
+        nc.gpsimd.memset(padded_e[:, 0:lead], 0.0)
+        nc.gpsimd.memset(padded_e[:, queries : lead + queries], 0.0)
+        nc.scalar.dma_start(padded_e[:, lead:queries], e)
+        margin = held.tile([queries, 1], F32)
+        nc.scalar.dma_start(margin[:], mg)
+
+        scores = [psum.tile([queries, PIECE], F32, name=f"scores{i}") for i in range(pieces)]
+        for b in range(blocks):
+            own_queries = padded_e[:, lead - b * QUERIES : lead - b * QUERIES + queries]
+            for i in range(pieces):
+                cols = slice(i * PIECE, (i + 1) * PIECE)
+                piece_list = lists[:, i * list_columns : (i + 1) * list_columns]
+                sums = ring.tile([P, PIECE], F32)
+                nc.vector.tensor_tensor(sums[:], tables[b][:].indirect(piece_list), corrections[b][:, cols], ADD)
+                rounded = ring.tile([P, PIECE], BF16)
+                nc.scalar.copy(rounded[:], sums[:])
+                nc.tensor.matmul(scores[i][:], own_queries, rounded[:], start=b == 0, stop=b == blocks - 1)
+
+        for i in range(pieces):
+            cols = slice(i * PIECE, (i + 1) * PIECE)
+            below = ring.tile([queries, PIECE], F32)
+            nc.scalar.activation(below[:], scores[i][:], RELU, bias=margin[:], scale=-1.0)
+            nc.sync.dma_start(out[:, cols], below[:])

@@ -40,28 +40,41 @@ def tile_lookup_adc_best_out_kernel(tc, tab, u, e, mg, offs, out):
             tables.append(table)
             corrections.append(correction)
 
-        lead = queries - QUERIES
-        padded_e = held.tile([P, lead + queries], BF16)
+        lead = P - QUERIES
+        padded_e = held.tile([P, lead + P], BF16)
         nc.gpsimd.memset(padded_e[:, 0:lead], 0.0)
-        nc.gpsimd.memset(padded_e[:, queries : lead + queries], 0.0)
-        nc.scalar.dma_start(padded_e[:, lead:queries], e)
-        margin = held.tile([queries, 1], F32)
-        nc.scalar.dma_start(margin[:], mg)
+        nc.gpsimd.memset(padded_e[:, P : lead + P], 0.0)
+        nc.scalar.dma_start(padded_e[:, lead:P], e)
+        margin = held.tile([P, 1], F32)
+        for h in range(2):
+            nc.scalar.dma_start(margin[h * queries : (h + 1) * queries, :], mg)
 
-        scores = [psum.tile([queries, PIECE], F32, name=f"scores{i}") for i in range(pieces)]
+        half = PIECE // 2
+        scores = [psum.tile([P, half], F32, name=f"scores{i}") for i in range(pieces)]
         for b in range(blocks):
-            own_queries = padded_e[:, lead - b * QUERIES : lead - b * QUERIES + queries]
             for i in range(pieces):
                 cols = slice(i * PIECE, (i + 1) * PIECE)
                 piece_list = lists[:, i * list_columns : (i + 1) * list_columns]
                 sums = ring.tile([P, PIECE], F32)
                 nc.vector.tensor_tensor(sums[:], tables[b][:].indirect(piece_list), corrections[b][:, cols], ADD)
                 rounded = ring.tile([P, PIECE], BF16)
-                nc.scalar.copy(rounded[:], sums[:])
-                nc.tensor.matmul(scores[i][:], own_queries, rounded[:], start=b == 0, stop=b == blocks - 1)
+                if b == blocks - 1 and i == pieces - 1:
+                    nc.vector.tensor_copy(rounded[:], sums[:])
+                else:
+                    nc.scalar.copy(rounded[:], sums[:])
+                for h in range(2):
+                    row = h * queries + b * QUERIES
+                    nc.tensor.matmul(
+                        scores[i][:],
+                        padded_e[:, lead - row : lead - row + P],
+                        rounded[:, h * half : (h + 1) * half],
+                        start=b == 0 and h == 0,
+                        stop=b == blocks - 1 and h == 1,
+                    )
 
         for i in range(pieces):
-            cols = slice(i * PIECE, (i + 1) * PIECE)
-            below = ring.tile([queries, PIECE], F32)
+            below = ring.tile([P, half], F32)
             nc.scalar.activation(below[:], scores[i][:], RELU, bias=margin[:], scale=-1.0)
-            nc.sync.dma_start(out[:, cols], below[:])
+            for h in range(2):
+                start = i * PIECE + h * half
+                nc.sync.dma_start(out[:, start : start + half], below[h * queries : (h + 1) * queries, :])

@@ -28,6 +28,11 @@ def tile_lookup_adc_best_out_kernel(tc, tab, u, e, mg, offs, out):
         lists = held.tile([P, vectors // 16], U16)
         nc.sync.dma_start(lists[:], offs)
 
+        lead = P - QUERIES
+        padded_e = held.tile([P, lead + P], BF16)
+        nc.gpsimd.memset(padded_e[:, 0:lead], 0.0)
+        nc.gpsimd.memset(padded_e[:, P : lead + P], 0.0)
+
         tables = []
         corrections = []
         for b in range(blocks):
@@ -39,15 +44,11 @@ def tile_lookup_adc_best_out_kernel(tc, tab, u, e, mg, offs, out):
                 nc.sync.dma_start(correction[:, cols], u[b * P : (b + 1) * P, cols])
             tables.append(table)
             corrections.append(correction)
-
-        lead = P - QUERIES
-        padded_e = held.tile([P, lead + P], BF16)
-        nc.gpsimd.memset(padded_e[:, 0:lead], 0.0)
-        nc.gpsimd.memset(padded_e[:, P : lead + P], 0.0)
-        nc.scalar.dma_start(padded_e[:, lead:P], e)
+            if b == 0:
+                nc.sync.dma_start(padded_e[:, lead:P], e)
         margin = held.tile([P, 1], F32)
         for h in range(2):
-            nc.scalar.dma_start(margin[h * queries : (h + 1) * queries, :], mg)
+            nc.sync.dma_start(margin[h * queries : (h + 1) * queries, :], mg)
 
         half = PIECE // 2
         scores = [psum.tile([P, half], F32, name=f"scores{i}") for i in range(pieces)]

@@ -60,7 +60,9 @@ def tile_lookup_adc_best_out_kernel(tc, tab, u, e, mg, offs, out):
                 nc.vector.tensor_tensor(sums[:], tables[b][:].indirect(piece_list), corrections[b][:, cols], ADD)
                 rounded = ring.tile([P, PIECE], BF16)
                 if b == blocks - 1 and i == pieces - 1:
-                    nc.vector.tensor_copy(rounded[:], sums[:])
+                    for h in range(2):
+                        part = slice(h * half, (h + 1) * half)
+                        nc.vector.tensor_copy(rounded[:, part], sums[:, part])
                 else:
                     nc.scalar.copy(rounded[:], sums[:])
                 for h in range(2):

import concourse.mybir as mybir

F32, BF16, U16 = mybir.dt.float32, mybir.dt.bfloat16, mybir.dt.uint16
ADD = mybir.AluOpType.add
RELU = mybir.ActivationFunctionType.Relu

P = 128
QUERIES = 16
PIECE = 512

FLOPS = 2 * 512 * 2048 + 2 * 64 * 2048


def tile_lookup_adc_best_out_kernel(tc, tab, u, e, mg, offs, out):
    nc = tc.nc
    rows, codewords = tab.shape
    vectors = u.shape[1]
    blocks = rows // P
    pieces = vectors // PIECE
    queries = blocks * QUERIES
    list_columns = PIECE // 16

    with (
        tc.tile_pool(name="held", bufs=1) as held,
        tc.tile_pool(name="ring", bufs=4) as ring,
        tc.psum_pool(name="psum", bufs=1) as psum,
    ):
        lists = held.tile([P, vectors // 16], U16)
        nc.sync.dma_start(lists[:], offs)

        lead = P - QUERIES
        padded_e = held.tile([P, lead + P], BF16)
        nc.gpsimd.memset(padded_e[:, 0:lead], 0.0)
        nc.gpsimd.memset(padded_e[:, P : lead + P], 0.0)

        tables = []
        corrections = []
        for b in range(blocks):
            table = held.tile([P, codewords], F32, name=f"table{b}")
            nc.sync.dma_start(table[:], tab[b * P : (b + 1) * P, :])
            correction = held.tile([P, vectors], F32, name=f"correction{b}")
            for i in range(pieces):
                cols = slice(i * PIECE, (i + 1) * PIECE)
                nc.sync.dma_start(correction[:, cols], u[b * P : (b + 1) * P, cols])
            tables.append(table)
            corrections.append(correction)
            if b == 0:
                nc.sync.dma_start(padded_e[:, lead:P], e)
        margin = held.tile([P, 1], F32)
        for h in range(2):
            nc.sync.dma_start(margin[h * queries : (h + 1) * queries, :], mg)

        half = PIECE // 2
        scores = [psum.tile([P, half], F32, name=f"scores{i}") for i in range(pieces)]
        for b in range(blocks):
            for i in range(pieces):
                cols = slice(i * PIECE, (i + 1) * PIECE)
                piece_list = lists[:, i * list_columns : (i + 1) * list_columns]
                sums = ring.tile([P, PIECE], F32)
                nc.vector.tensor_tensor(sums[:], tables[b][:].indirect(piece_list), corrections[b][:, cols], ADD)
                rounded = ring.tile([P, PIECE], BF16)
                if b == blocks - 1 and i == pieces - 1:
                    for h in range(2):
                        part = slice(h * half, (h + 1) * half)
                        nc.vector.tensor_copy(rounded[:, part], sums[:, part])
                else:
                    nc.scalar.copy(rounded[:], sums[:])
                for h in range(2):
                    row = h * queries + b * QUERIES
                    nc.tensor.matmul(
                        scores[i][:],
                        padded_e[:, lead - row : lead - row + P],
                        rounded[:, h * half : (h + 1) * half],
                        start=b == 0 and h == 0,
                        stop=b == blocks - 1 and h == 1,
                    )

        for i in range(pieces):
            below = ring.tile([P, half], F32)
            nc.scalar.activation(below[:], scores[i][:], RELU, bias=margin[:], scale=-1.0)
            for h in range(2):
                start = i * PIECE + h * half
                nc.sync.dma_start(out[:, start : start + half], below[h * queries : (h + 1) * queries, :])
